import numpy as np
import ml_dtypes


def mxq(x, axis, fmt="e4m3"):
    dtype, down = {"e4m3": (ml_dtypes.float8_e4m3fn, 7), "e5m2": (ml_dtypes.float8_e5m2, 14)}[fmt]
    v = np.moveaxis(np.asarray(x, np.float32).astype(ml_dtypes.bfloat16).astype(np.float64), axis, -1)
    blocks = v.reshape(v.shape[:-1] + (-1, 32))
    amax = np.abs(blocks).max(-1, keepdims=True)
    byte = np.maximum(np.where(amax > 0, np.frexp(amax)[1] - 1 + 127, 0) - down, 1)
    scale = np.exp2(byte - 127.0)
    codes = (blocks / scale).astype(np.float32).astype(dtype).astype(np.float64)
    return np.moveaxis((codes * scale).reshape(v.shape), -1, axis)


WIDE = False


def mx_kscale(k):
    if not WIDE:
        return np.ones(k)
    levels = np.array([10, -10, 5, -5, 0])
    if k % 512:
        return np.exp2(np.random.permutation(np.resize(levels, k // 32))).repeat(32)
    a = np.empty((k // 512, 16))
    for p in range(k // 512):
        a[p, :8] = np.random.permutation(np.resize(levels, 8))
        for g in range(8):
            far = levels[np.abs(levels - a[p, g]) >= 10]
            a[p, g + 8] = far[np.random.randint(len(far))]
    return np.exp2(a.ravel()).repeat(32)


def f64(x):
    return np.asarray(x).astype(np.float64)


def striped(idx):
    return np.tile(idx.reshape(-1, 16).T, (8, 1)).astype(np.uint16)


def unstriped(offs):
    return offs[:16].T.reshape(-1).astype(np.int64)


E2M1 = np.array([0.0, 0.5, 1.0, 1.5, 2.0, 3.0, 4.0, 6.0, -0.0, -0.5, -1.0, -1.5, -2.0, -3.0, -4.0, -6.0])


def pack_weight(w, fmt):
    k, n = w.shape
    w = f64(np.asarray(w, np.float32).astype(ml_dtypes.bfloat16)).reshape(k // 32, 32, n)
    amax = np.abs(w).max(1)
    if fmt == "e4m3":
        byte = np.frexp(amax)[1] - 1 + 127 - 7
    else:
        mant, ex = np.frexp(amax / 6.0)
        byte = np.where(mant > 0.5, ex, ex - 1) + 127
    byte = np.clip(np.where(amax > 0, byte, 1), 1, 254)
    scaled = (w * np.exp2(127.0 - byte)[:, None, :]).reshape(k, n).astype(np.float32)
    by_word = np.ascontiguousarray(scaled.reshape(k // 512, 128, 4, n).transpose(0, 1, 3, 2))
    if fmt == "e4m3":
        words = by_word.astype(ml_dtypes.float8_e4m3fn).view(np.uint8)
    else:
        c = by_word.astype(ml_dtypes.float4_e2m1fn).view(np.uint8) & 0xF
        words = (c[..., 0::2] | (c[..., 1::2] << 4)).reshape(k // 512, 128, 2 * n)
    return np.ascontiguousarray(words), np.ascontiguousarray(byte.astype(np.uint8).reshape(k // 512, 16, n))


def unpack_weight(words, scales, fmt):
    g, _, n = scales.shape
    words = np.ascontiguousarray(words).reshape(g, 128, n, -1)
    if fmt == "e4m3":
        vals = words.view(ml_dtypes.float8_e4m3fn).astype(np.float64)
    else:
        nib = np.empty((g, 128, n, 4), np.uint8)
        nib[..., 0::2] = words & 0xF
        nib[..., 1::2] = words >> 4
        vals = E2M1[nib]
    vals = vals * np.repeat(np.exp2(scales.astype(np.float64) - 127.0), 8, axis=1)[..., None]
    return vals.transpose(0, 1, 3, 2).reshape(g * 512, n)


def gelu(v):
    return 0.5 * v * (1.0 + np.tanh(np.sqrt(2.0 / np.pi) * (v + 0.044715 * v**3)))


def often(T, S):
    return np.random.permutation(T)[(T * np.random.uniform(0, 1, S) ** 4).astype(np.int64)]


K, K2, K3, T, S, H, N, P = 1024, 512, 512, 2048, 1024, 1024, 384, 512

def setup_inputs():
    n = np.random.standard_normal
    s, s2, s3 = mx_kscale(K)[:, None], mx_kscale(K2)[:, None], mx_kscale(K3)[:, None]
    u = mx_kscale(H)[:, None]
    d = {}
    d["tab_words"], d["tab_scales"] = pack_weight(n((K, T)) * s, "e4m3")
    d["tab2_words"], d["tab2_scales"] = pack_weight(n((K2, T)) * s2, "e4m3")
    d["tab3_words"], d["tab3_scales"] = pack_weight(n((K3, T)) * s3, "e4m3")
    d["offs"] = striped(np.random.permutation(T)[:S])
    d["offs2"] = striped(np.random.permutation(T)[:S])
    d["offs3"] = striped(np.random.permutation(T)[:S])
    d["pos1"] = striped(np.random.permutation(S)[:P])
    d["pos2"] = striped(often(S, P))
    d["pos3"] = striped(often(S, P))
    d["w1"] = (2.0 * n((K, H)) / K ** 0.5 / s).astype(np.float32)
    d["w2_words"], d["w2_scales"] = pack_weight(0.7 * n((K2, H)) / K2 ** 0.5 / s2, "e2m1")
    d["w3"] = (0.8 * n((K3, H)) / K3 ** 0.5 / s3).astype(np.float32)
    d["gain"] = (np.random.uniform(0.5, 1.5, H) * u[:, 0]).astype(np.float32)
    d["w4_words"], d["w4_scales"] = pack_weight(0.25 * n((H, N)) / H ** 0.5 / u, "e4m3")
    d["phase"] = np.random.uniform(-1.2, 1.2, N).astype(np.float32)
    return d

def reference(tab_words, tab_scales, tab2_words, tab2_scales, tab3_words, tab3_scales,
              offs, offs2, offs3, pos1, pos2, pos3, w1, w2_words, w2_scales, w3, gain,
              w4_words, w4_scales, phase):
    v = unpack_weight(tab_words, tab_scales, "e4m3")[:, unstriped(offs)]
    v2 = unpack_weight(tab2_words, tab2_scales, "e4m3")[:, unstriped(offs2)]
    v3 = unpack_weight(tab3_words, tab3_scales, "e4m3")[:, unstriped(offs3)]
    a = mxq(f64(w1), 0, "e4m3").T @ v
    b = unpack_weight(w2_words, w2_scales, "e2m1").T @ v2
    d = mxq(f64(w3), 0, "e4m3").T @ v3
    z = np.tanh(a[:, unstriped(pos1)]) - b[:, unstriped(pos2)] + np.square(d[:, unstriped(pos3)])
    z = z * f64(gain)[:, None]
    y = unpack_weight(w4_words, w4_scales, "e4m3").T @ mxq(z, 0, "e4m3")
    return np.cos(y + f64(phase)[:, None])

@@ -1,0 +1,257 @@
+import math
+from contextlib import ExitStack
+
+import concourse.mybir as mybir
+
+K, K2, K3, T, S, H, N, J = 1024, 512, 512, 2048, 1024, 1024, 384, 512
+FLOPS = 2 * (K + K2 + K3) * H * S + 2 * H * N * J
+
+F32 = mybir.dt.float32
+BF16 = mybir.dt.bfloat16
+I32 = mybir.dt.int32
+U32 = mybir.dt.uint32
+U16 = mybir.dt.uint16
+U8 = mybir.dt.uint8
+FP8X4 = mybir.dt.float8_e4m3fn_x4
+FP4X4 = mybir.dt.float4_e2m1fn_x4
+ACT = mybir.ActivationFunctionType
+ALU = mybir.AluOpType
+
+P = 128
+PACK = 4
+PASS = P * PACK
+BANK = 512
+HALF = J // 2
+TURN = 1.0 / (2.0 * math.pi)
+SHIFT = 3.0
+
+
+def tile_list_hologram_label_phase_kernel(
+    tc, tab_words, tab_scales, tab2_words, tab2_scales, tab3_words, tab3_scales,
+    offs, offs2, offs3, pos1, pos2, pos3, w1, w2_words, w2_scales, w3, gain,
+    w4_words, w4_scales, phase, out,
+):
+    nc = tc.nc
+    with ExitStack() as ctx:
+        keep = ctx.enter_context(tc.tile_pool(name="keep", bufs=1))
+        ring = ctx.enter_context(tc.tile_pool(name="ring", bufs=3))
+        psum = ctx.enter_context(tc.psum_pool(name="psum", bufs=8))
+
+        def held(shape, dtype, name):
+            return keep.tile(shape, dtype, name=name, align_bytes=64)
+
+        def load_list(dram, name):
+            lst = keep.tile(list(dram.shape), U16, name=name)
+            nc.sync.dma_start(lst[:], dram)
+            return lst
+
+        def zeroed_plane(engine, width, name):
+            plane = held([P, width], U8, name)
+            engine.memset(plane[:].bitcast(I32), 0)
+            return plane
+
+        def load_plane(queue, plane, scales):
+            passes = scales.shape[0]
+            for q in range(4):
+                rows = scales[:, 4 * q : 4 * q + 4, :] if passes > 1 else scales[0, 4 * q : 4 * q + 4, :]
+                queue.dma_start(plane[32 * q : 32 * q + 4 * passes, :].bitcast(I32), rows.bitcast(I32))
+
+        def load_words(words, a, name):
+            tile = keep.tile([P, T], U32, name=name, tag=name, align_bytes=64)
+            nc.sync.dma_start(tile[:].bitcast(I32), words[a].rearrange("p t i -> p (t i)").bitcast(I32))
+            return tile
+
+        def load_weight(w, a, b, name):
+            raw = keep.tile([P, PACK, PASS], F32, name=name, tag=name)
+            rows = w[a * PASS : (a + 1) * PASS, b * PASS : (b + 1) * PASS]
+            nc.sync.dma_start(raw[:], rows.rearrange("(p j) c -> p j c", j=PACK))
+            return raw
+
+        def gather_bytes(window, lst, dtype, name):
+            picked = held([P, S], dtype, name)
+            nc.vector.tensor_copy(picked[:], window[:].indirect(lst[:]))
+            return picked
+
+        def quantise_weight(raw, name):
+            grouped = ring.tile([P, PASS * PACK], BF16, name="grouped", align_bytes=64)
+            nc.scalar.copy(
+                grouped[:].rearrange("p (t m j) -> p m j t", t=PACK, j=PACK),
+                raw[:].rearrange("p j (m t) -> p m j t", t=PACK),
+            )
+            codes = held([P, PASS], U32, name + "_codes")
+            plane = held([P, PASS], U8, name + "_plane")
+            nc.vector.quantize_mx(codes[:].bitcast(FP8X4), plane[:], grouped[:])
+            return codes, plane
+
+        def first_stage(passes, func, bias, window=None):
+            if window is None:
+                window = ring.tile([P, S], F32, name="window", bufs=8)
+            for h in range(S // BANK):
+                cols = slice(h * BANK, (h + 1) * BANK)
+                acc = psum.tile([P, BANK], F32, name="acc")
+                for a, (lhs, lhs_plane, words, plane) in enumerate(passes):
+                    nc.tensor.matmul_mx(
+                        acc[:], lhsT=lhs, lhsT_scale=lhs_plane,
+                        rhs=words[:, cols].bitcast(FP8X4), rhs_scale=plane[4 * a :, cols],
+                        start=(a == 0), stop=(a == len(passes) - 1),
+                    )
+                nc.scalar.activation(window[:, cols], acc[:], func, bias=bias)
+            return window
+
+        plane2 = zeroed_plane(nc.vector, T, "plane2")
+        w2_plane_raw = zeroed_plane(nc.vector, H, "w2_plane_raw")
+        plane3 = zeroed_plane(nc.vector, T, "plane3")
+        plane1 = zeroed_plane(nc.gpsimd, T, "plane1")
+        w4_plane = zeroed_plane(nc.gpsimd, N, "w4_plane")
+        zero_in = keep.tile([P, 1], F32, name="zero_in")
+        nc.vector.memset(zero_in[:], 0.0)
+        zero = keep.tile([P, 1], F32, name="zero")
+        nc.scalar.activation(zero[:], zero_in[:], ACT.Silu)
+
+        list2 = load_list(offs2, "list2")
+        w2_raw = held([P, 2 * H], U8, "w2_raw")
+        nc.sync.dma_start(w2_raw[:].bitcast(I32), w2_words[0].bitcast(I32))
+        list3 = load_list(offs3, "list3")
+        words2 = load_words(tab2_words, 0, "words2")
+        load_plane(nc.sync, plane2, tab2_scales)
+        raw3 = [load_weight(w3, 0, 0, "raw3_0")]
+        load_plane(nc.sync, w2_plane_raw, w2_scales)
+        raw3.append(load_weight(w3, 0, 1, "raw3_1"))
+        load_plane(nc.sync, plane3, tab3_scales)
+        words3 = load_words(tab3_words, 0, "words3")
+        places2 = load_list(pos2, "places2")
+        list1 = load_list(offs, "list1")
+        load_plane(nc.sync, plane1, tab_scales)
+        raw1 = {(0, 0): load_weight(w1, 0, 0, "raw1_00")}
+        words1 = [load_words(tab_words, a, f"words1_{a}") for a in range(2)]
+        places3 = load_list(pos3, "places3")
+        raw1[1, 0] = load_weight(w1, 1, 0, "raw1_10")
+        places1 = load_list(pos1, "places1")
+        gains = keep.tile([P, 2, PACK], F32, name="gains")
+        nc.sync.dma_start(gains[:], gain.rearrange("(b p t) -> p b t", b=2, t=PACK))
+        for a in range(2):
+            raw1[a, 1] = load_weight(w1, a, 1, f"raw1_{a}1")
+        w4_codes = held([P, 2, N], U32, "w4_codes")
+        nc.sync.dma_start(w4_codes[:].bitcast(I32), w4_words.rearrange("a p n i -> p a (n i)").bitcast(I32))
+        load_plane(nc.sync, w4_plane, w4_scales)
+        phases = keep.tile([P, N // P], F32, name="phases")
+        with nc.allow_non_contiguous_dma(reason="one phase a partition"):
+            nc.sync.dma_start(phases[:], phase.rearrange("(i p) -> p i", p=P))
+
+        w2_codes = held([P, 2 * H], U8, "w2_codes")
+        nc.vector.tensor_copy(
+            w2_codes[:].bitcast(U16).rearrange("p (b t q) -> p b q t", b=2, t=PACK),
+            w2_raw[:].bitcast(U16).rearrange("p (b q t) -> p b q t", b=2, t=PACK),
+        )
+        picked2 = gather_bytes(words2, list2, U32, "picked2")
+        picked_plane2 = gather_bytes(plane2, list2, U8, "picked_plane2")
+        w2_plane = held([P, H], U8, "w2_plane")
+        nc.vector.tensor_copy(
+            w2_plane[:].rearrange("p (b t q) -> p b q t", b=2, t=PACK),
+            w2_plane_raw[:].rearrange("p (b q t) -> p b q t", b=2, t=PACK),
+        )
+        picked_plane3 = gather_bytes(plane3, list3, U8, "picked_plane3")
+        quant3 = [quantise_weight(raw3[b], f"w3_{b}") for b in range(2)]
+        picked3 = gather_bytes(words3, list3, U32, "picked3")
+        picked_plane1 = gather_bytes(plane1, list1, U8, "picked_plane1")
+        picked1 = [gather_bytes(words1[a], list1, U32, f"picked1_{a}") for a in range(2)]
+
+        slices = [(b, t) for b in range(2) for t in range(PACK)]
+
+        def cols_of(t):
+            return slice(t * P, (t + 1) * P)
+
+        part_b = [keep.tile([P, PACK, J], F32, name=f"part_b{b}", tag=tag, align_bytes=64) for b, tag in enumerate(("words3", "words1_0"))]
+        for b, t in slices:
+            c0 = b * PASS + t * P
+            window = first_stage(
+                [(w2_codes[:, 2 * c0 : 2 * (c0 + P)].bitcast(FP4X4), w2_plane[:, c0 : c0 + P], picked2, picked_plane2)],
+                ACT.Copy, 0.0,
+                keep.tile([P, S], F32, name="first_window", tag="raw3_1") if c0 == 0 else None,
+            )
+            nc.vector.tensor_copy(part_b[b][:, t, :], window[:].indirect(places2[:]))
+
+        part_d = [keep.tile([P, PACK, J], F32, name=f"part_d{b}", tag=tag, align_bytes=64) for b, tag in enumerate(("words1_1", "words2"))]
+        quant1 = {}
+        for b, t in slices:
+            codes, plane = quant3[b]
+            window = first_stage(
+                [(codes[:, cols_of(t)].bitcast(FP8X4), plane[:, cols_of(t)], picked3, picked_plane3)],
+                ACT.Square, 0.0,
+            )
+            nc.vector.tensor_tensor(part_d[b][:, t, :], window[:].indirect(places3[:]), part_b[b][:, t, :], ALU.subtract)
+            if t == PACK - 1:
+                for a in range(2):
+                    quant1[a, b] = quantise_weight(raw1[a, b], f"w1_{a}{b}")
+
+        def a_window(b, t):
+            return first_stage(
+                [(quant1[a, b][0][:, cols_of(t)].bitcast(FP8X4), quant1[a, b][1][:, cols_of(t)], picked1[a], picked_plane1)
+                 for a in range(2)],
+                ACT.Tanh, zero[:],
+            )
+
+        sums0 = keep.tile([P, PACK, J], F32, name="sums0")
+        for t in range(PACK):
+            window = a_window(0, t)
+            nc.vector.tensor_tensor(sums0[:, t, :], window[:].indirect(places1[:]), part_d[0][:, t, :], ALU.add)
+        windows1 = [a_window(1, t) for t in range(PACK)]
+
+        scaled0 = held([P, PACK, J], BF16, "scaled0")
+        for t in range(PACK):
+            nc.scalar.activation(scaled0[:, t, :], sums0[:, t, :], ACT.Copy, scale=gains[:, 0, t : t + 1])
+        z0 = held([P, J * PACK], BF16, "z0")
+        nc.scalar.copy(
+            z0[:].rearrange("p (c i t) -> p c t i", i=4, t=PACK),
+            scaled0[:].rearrange("p t (c i) -> p c t i", i=4),
+        )
+        z0_codes = held([P, J], U32, "z0_codes")
+        z0_plane = held([P, J], U8, "z0_plane")
+        nc.vector.quantize_mx(z0_codes[:].bitcast(FP8X4), z0_plane[:], z0[:])
+
+        turns = keep.tile([P, N // P], F32, name="turns")
+        nc.vector.tensor_scalar(turns[:], phases[:], TURN, SHIFT, ALU.mult, ALU.add)
+
+        z1 = []
+        for h in range(2):
+            cols = slice(h * HALF, (h + 1) * HALF)
+            sums1 = keep.tile([P, PACK, HALF], F32, name=f"sums1_{h}")
+            for t in range(PACK):
+                nc.vector.tensor_tensor(
+                    sums1[:, t, :], windows1[t][:].indirect(places1[:, h * HALF // 16 : (h + 1) * HALF // 16]),
+                    part_d[1][:, t, cols], ALU.add,
+                )
+            z = held([P, HALF * PACK], BF16, f"z1_{h}")
+            nc.vector.tensor_tensor(
+                z[:].rearrange("p (c i t) -> p c t i", i=4, t=PACK),
+                sums1[:].rearrange("p t (c i) -> p c t i", i=4),
+                gains[:, 1, :].unsqueeze(1).unsqueeze(3).to_broadcast([P, HALF // 4, PACK, 4]),
+                ALU.mult,
+            )
+            codes = held([P, HALF], U32, f"z1_codes_{h}")
+            plane = held([P, HALF], U8, f"z1_plane_{h}")
+            nc.vector.quantize_mx(codes[:].bitcast(FP8X4), plane[:], z[:])
+            z1.append((codes, plane))
+
+        for h in range(2):
+            cols = slice(h * HALF, (h + 1) * HALF)
+            for i in range(N // P):
+                acc = psum.tile([P, BANK], F32, name="acc")
+                y = acc[:, :HALF]
+                nc.tensor.matmul_mx(
+                    y, lhsT=w4_codes[:, 0, cols_of(i)].bitcast(FP8X4), lhsT_scale=w4_plane[:, cols_of(i)],
+                    rhs=z0_codes[:, cols].bitcast(FP8X4), rhs_scale=z0_plane[:, cols], start=True, stop=False,
+                )
+                nc.tensor.matmul_mx(
+                    y, lhsT=w4_codes[:, 1, cols_of(i)].bitcast(FP8X4), lhsT_scale=w4_plane[4:, cols_of(i)],
+                    rhs=z1[h][0][:].bitcast(FP8X4), rhs_scale=z1[h][1][:], start=False, stop=True,
+                )
+                whole = ring.tile([P, HALF], I32, name="whole")
+                nc.vector.tensor_scalar(whole[:], y, TURN, turns[:, i : i + 1], ALU.mult, ALU.add)
+                rest = ring.tile([P, HALF], F32, name="rest")
+                nc.vector.scalar_tensor_tensor(rest[:], y, TURN, whole[:], ALU.mult, ALU.subtract)
+                size = ring.tile([P, HALF], F32, name="size")
+                nc.scalar.activation(size[:], rest[:], ACT.Abs, bias=turns[:, i : i + 1])
+                result = ring.tile([P, HALF], F32, name="result")
+                nc.scalar.activation(result[:], size[:], ACT.Sin, bias=math.pi / 2, scale=-2.0 * math.pi)
+                nc.sync.dma_start(out[cols_of(i), cols], result[:])

@@ -23,7 +23,7 @@ PASS = P * PACK
 BANK = 512
 HALF = J // 2
 TURN = 1.0 / (2.0 * math.pi)
-SHIFT = 3.0
+QUARTER = 0.25
 
 
 def tile_list_hologram_label_phase_kernel(
@@ -35,10 +35,11 @@ def tile_list_hologram_label_phase_kernel(
     with ExitStack() as ctx:
         keep = ctx.enter_context(tc.tile_pool(name="keep", bufs=1))
         ring = ctx.enter_context(tc.tile_pool(name="ring", bufs=3))
+        stage = ctx.enter_context(tc.tile_pool(name="stage", bufs=1))
         psum = ctx.enter_context(tc.psum_pool(name="psum", bufs=8))
 
-        def held(shape, dtype, name):
-            return keep.tile(shape, dtype, name=name, align_bytes=64)
+        def held(shape, dtype, name, tag=None):
+            return keep.tile(shape, dtype, name=name, tag=tag or name, align_bytes=64)
 
         def load_list(dram, name):
             lst = keep.tile(list(dram.shape), U16, name=name)
@@ -61,8 +62,8 @@ def tile_list_hologram_label_phase_kernel(
             nc.sync.dma_start(tile[:].bitcast(I32), words[a].rearrange("p t i -> p (t i)").bitcast(I32))
             return tile
 
-        def load_weight(w, a, b, name):
-            raw = keep.tile([P, PACK, PASS], F32, name=name, tag=name)
+        def load_weight(w, a, b, name, place):
+            raw = stage.tile([P, PACK, PASS], F32, name=name, offset=place * 2 * 4 * S)
             rows = w[a * PASS : (a + 1) * PASS, b * PASS : (b + 1) * PASS]
             nc.sync.dma_start(raw[:], rows.rearrange("(p j) c -> p j c", j=PACK))
             return raw
@@ -72,13 +73,13 @@ def tile_list_hologram_label_phase_kernel(
             nc.vector.tensor_copy(picked[:], window[:].indirect(lst[:]))
             return picked
 
-        def quantise_weight(raw, name):
-            grouped = ring.tile([P, PASS * PACK], BF16, name="grouped", align_bytes=64)
+        def quantise_weight(raw, name, grouped_tag, tag=None):
+            grouped = held([P, PASS * PACK], BF16, name + "_grouped", grouped_tag)
             nc.scalar.copy(
                 grouped[:].rearrange("p (t m j) -> p m j t", t=PACK, j=PACK),
                 raw[:].rearrange("p j (m t) -> p m j t", t=PACK),
             )
-            codes = held([P, PASS], U32, name + "_codes")
+            codes = held([P, PASS], U32, name + "_codes", tag)
             plane = held([P, PASS], U8, name + "_plane")
             nc.vector.quantize_mx(codes[:].bitcast(FP8X4), plane[:], grouped[:])
             return codes, plane
@@ -98,11 +99,10 @@ def tile_list_hologram_label_phase_kernel(
                 nc.scalar.activation(window[:, cols], acc[:], func, bias=bias)
             return window
 
-        plane2 = zeroed_plane(nc.vector, T, "plane2")
         w2_plane_raw = zeroed_plane(nc.vector, H, "w2_plane_raw")
         plane3 = zeroed_plane(nc.vector, T, "plane3")
-        plane1 = zeroed_plane(nc.gpsimd, T, "plane1")
-        w4_plane = zeroed_plane(nc.gpsimd, N, "w4_plane")
+        plane1 = zeroed_plane(nc.vector, T, "plane1")
+        w4_plane = zeroed_plane(nc.vector, N, "w4_plane")
         zero_in = keep.tile([P, 1], F32, name="zero_in")
         nc.vector.memset(zero_in[:], 0.0)
         zero = keep.tile([P, 1], F32, name="zero")
@@ -111,26 +111,27 @@ def tile_list_hologram_label_phase_kernel(
         list2 = load_list(offs2, "list2")
         w2_raw = held([P, 2 * H], U8, "w2_raw")
         nc.sync.dma_start(w2_raw[:].bitcast(I32), w2_words[0].bitcast(I32))
-        list3 = load_list(offs3, "list3")
+        plane2 = held([P, T], U8, "plane2")
+        for q in range(4):
+            rows = tab2_scales[0, 4 * q : 4 * q + 4, :].bitcast(I32)
+            nc.sync.dma_start(plane2[32 * q : 32 * q + 32, :].bitcast(I32), rows.unsqueeze(0).to_broadcast([8, 4, T // 4]))
         words2 = load_words(tab2_words, 0, "words2")
-        load_plane(nc.sync, plane2, tab2_scales)
-        raw3 = [load_weight(w3, 0, 0, "raw3_0")]
+        raw3 = [load_weight(w3, 0, 0, "raw3_0", 0)]
         load_plane(nc.sync, w2_plane_raw, w2_scales)
-        raw3.append(load_weight(w3, 0, 1, "raw3_1"))
+        list3 = load_list(offs3, "list3")
+        raw3.append(load_weight(w3, 0, 1, "raw3_1", 1))
         load_plane(nc.sync, plane3, tab3_scales)
         words3 = load_words(tab3_words, 0, "words3")
         places2 = load_list(pos2, "places2")
         list1 = load_list(offs, "list1")
         load_plane(nc.sync, plane1, tab_scales)
-        raw1 = {(0, 0): load_weight(w1, 0, 0, "raw1_00")}
-        words1 = [load_words(tab_words, a, f"words1_{a}") for a in range(2)]
+        words1 = [load_words(tab_words, 0, "words1_0")]
         places3 = load_list(pos3, "places3")
-        raw1[1, 0] = load_weight(w1, 1, 0, "raw1_10")
+        words1.append(load_words(tab_words, 1, "words1_1"))
+        raw1 = {(a, b): load_weight(w1, a, b, f"raw1_{a}{b}", 2 + 2 * b + a) for b in range(2) for a in range(2)}
         places1 = load_list(pos1, "places1")
         gains = keep.tile([P, 2, PACK], F32, name="gains")
         nc.sync.dma_start(gains[:], gain.rearrange("(b p t) -> p b t", b=2, t=PACK))
-        for a in range(2):
-            raw1[a, 1] = load_weight(w1, a, 1, f"raw1_{a}1")
         w4_codes = held([P, 2, N], U32, "w4_codes")
         nc.sync.dma_start(w4_codes[:].bitcast(I32), w4_words.rearrange("a p n i -> p a (n i)").bitcast(I32))
         load_plane(nc.sync, w4_plane, w4_scales)
@@ -143,15 +144,15 @@ def tile_list_hologram_label_phase_kernel(
             w2_codes[:].bitcast(U16).rearrange("p (b t q) -> p b q t", b=2, t=PACK),
             w2_raw[:].bitcast(U16).rearrange("p (b q t) -> p b q t", b=2, t=PACK),
         )
-        picked2 = gather_bytes(words2, list2, U32, "picked2")
         picked_plane2 = gather_bytes(plane2, list2, U8, "picked_plane2")
+        picked2 = gather_bytes(words2, list2, U32, "picked2")
         w2_plane = held([P, H], U8, "w2_plane")
         nc.vector.tensor_copy(
             w2_plane[:].rearrange("p (b t q) -> p b q t", b=2, t=PACK),
             w2_plane_raw[:].rearrange("p (b q t) -> p b q t", b=2, t=PACK),
         )
         picked_plane3 = gather_bytes(plane3, list3, U8, "picked_plane3")
-        quant3 = [quantise_weight(raw3[b], f"w3_{b}") for b in range(2)]
+        quant3 = [quantise_weight(raw3[b], f"w3_{b}", f"grouped{b}", tag) for b, tag in enumerate(("w2_plane_raw", "plane3"))]
         picked3 = gather_bytes(words3, list3, U32, "picked3")
         picked_plane1 = gather_bytes(plane1, list1, U8, "picked_plane1")
         picked1 = [gather_bytes(words1[a], list1, U32, f"picked1_{a}") for a in range(2)]
@@ -167,50 +168,60 @@ def tile_list_hologram_label_phase_kernel(
             window = first_stage(
                 [(w2_codes[:, 2 * c0 : 2 * (c0 + P)].bitcast(FP4X4), w2_plane[:, c0 : c0 + P], picked2, picked_plane2)],
                 ACT.Copy, 0.0,
-                keep.tile([P, S], F32, name="first_window", tag="raw3_1") if c0 == 0 else None,
+                stage.tile([P, S], F32, name="first_window", offset=2 * 4 * S) if c0 == 0 else None,
             )
             nc.vector.tensor_copy(part_b[b][:, t, :], window[:].indirect(places2[:]))
 
-        part_d = [keep.tile([P, PACK, J], F32, name=f"part_d{b}", tag=tag, align_bytes=64) for b, tag in enumerate(("words1_1", "words2"))]
-        quant1 = {}
+        windows_d = []
         for b, t in slices:
             codes, plane = quant3[b]
-            window = first_stage(
+            windows_d.append(first_stage(
                 [(codes[:, cols_of(t)].bitcast(FP8X4), plane[:, cols_of(t)], picked3, picked_plane3)],
                 ACT.Square, 0.0,
-            )
-            nc.vector.tensor_tensor(part_d[b][:, t, :], window[:].indirect(places3[:]), part_b[b][:, t, :], ALU.subtract)
-            if t == PACK - 1:
-                for a in range(2):
-                    quant1[a, b] = quantise_weight(raw1[a, b], f"w1_{a}{b}")
+            ))
+        quant1 = {}
+        part_d = {}
+        for pair, tag in enumerate(("words1_1", "grouped1", "grouped2", "grouped3")):
+            both = held([P, 2, J], F32, f"part_d{pair}", tag)
+            for e in range(2):
+                b, t = slices[2 * pair + e]
+                part_d[b, t] = both[:, e, :]
+                nc.vector.tensor_tensor(part_d[b, t], windows_d[2 * pair + e][:].indirect(places3[:]), part_b[b][:, t, :], ALU.subtract)
+            for a, b in (((0, 0), (1, 0)), ((0, 1),), ((1, 1),), ())[pair]:
+                quant1[a, b] = quantise_weight(raw1[a, b], f"w1_{a}{b}", f"grouped{2 * b + a}")
 
         def a_window(b, t):
             return first_stage(
                 [(quant1[a, b][0][:, cols_of(t)].bitcast(FP8X4), quant1[a, b][1][:, cols_of(t)], picked1[a], picked_plane1)
                  for a in range(2)],
                 ACT.Tanh, zero[:],
+                stage.tile([P, S], F32, name=f"window_a{b}{t}", offset=(10 - 4 * b - 2 * (t // 2) + t % 2) * 4 * S),
             )
 
         sums0 = keep.tile([P, PACK, J], F32, name="sums0")
         for t in range(PACK):
             window = a_window(0, t)
-            nc.vector.tensor_tensor(sums0[:, t, :], window[:].indirect(places1[:]), part_d[0][:, t, :], ALU.add)
+            nc.vector.tensor_tensor(sums0[:, t, :], window[:].indirect(places1[:]), part_d[0, t], ALU.add)
         windows1 = [a_window(1, t) for t in range(PACK)]
 
-        scaled0 = held([P, PACK, J], BF16, "scaled0")
-        for t in range(PACK):
-            nc.scalar.activation(scaled0[:, t, :], sums0[:, t, :], ACT.Copy, scale=gains[:, 0, t : t + 1])
-        z0 = held([P, J * PACK], BF16, "z0")
-        nc.scalar.copy(
-            z0[:].rearrange("p (c i t) -> p c t i", i=4, t=PACK),
-            scaled0[:].rearrange("p t (c i) -> p c t i", i=4),
-        )
+        def z_on_scalar(sums, b, width, name):
+            scaled = held([P, PACK, width], BF16, name + "_scaled")
+            for t in range(PACK):
+                nc.scalar.activation(scaled[:, t, :], sums[:, t, :], ACT.Copy, scale=gains[:, b, t : t + 1])
+            z = held([P, width * PACK], BF16, name)
+            nc.scalar.copy(
+                z[:].rearrange("p (c i t) -> p c t i", i=4, t=PACK),
+                scaled[:].rearrange("p t (c i) -> p c t i", i=4),
+            )
+            return z
+
+        z0 = z_on_scalar(sums0, 0, J, "z0")
         z0_codes = held([P, J], U32, "z0_codes")
         z0_plane = held([P, J], U8, "z0_plane")
         nc.vector.quantize_mx(z0_codes[:].bitcast(FP8X4), z0_plane[:], z0[:])
 
         turns = keep.tile([P, N // P], F32, name="turns")
-        nc.vector.tensor_scalar(turns[:], phases[:], TURN, SHIFT, ALU.mult, ALU.add)
+        nc.vector.tensor_scalar(turns[:], phases[:], TURN, QUARTER, ALU.mult, ALU.add)
 
         z1 = []
         for h in range(2):
@@ -219,19 +230,34 @@ def tile_list_hologram_label_phase_kernel(
             for t in range(PACK):
                 nc.vector.tensor_tensor(
                     sums1[:, t, :], windows1[t][:].indirect(places1[:, h * HALF // 16 : (h + 1) * HALF // 16]),
-                    part_d[1][:, t, cols], ALU.add,
+                    part_d[1, t][:, cols], ALU.add,
                 )
-            z = held([P, HALF * PACK], BF16, f"z1_{h}")
-            nc.vector.tensor_tensor(
-                z[:].rearrange("p (c i t) -> p c t i", i=4, t=PACK),
-                sums1[:].rearrange("p t (c i) -> p c t i", i=4),
-                gains[:, 1, :].unsqueeze(1).unsqueeze(3).to_broadcast([P, HALF // 4, PACK, 4]),
-                ALU.mult,
-            )
+            if h == 0:
+                z = z_on_scalar(sums1, 1, HALF, "z1_0")
+            else:
+                z = held([P, HALF * PACK], BF16, f"z1_{h}")
+                nc.vector.tensor_tensor(
+                    z[:].rearrange("p (c i t) -> p c t i", i=4, t=PACK),
+                    sums1[:].rearrange("p t (c i) -> p c t i", i=4),
+                    gains[:, 1, :].unsqueeze(1).unsqueeze(3).to_broadcast([P, HALF // 4, PACK, 4]),
+                    ALU.mult,
+                )
             codes = held([P, HALF], U32, f"z1_codes_{h}")
             plane = held([P, HALF], U8, f"z1_plane_{h}")
             nc.vector.quantize_mx(codes[:].bitcast(FP8X4), plane[:], z[:])
             z1.append((codes, plane))
+
+        angle = held([P, 2, N // P, HALF], F32, "angle", "words2")
+        whole = held([P, 2, N // P, HALF], I32, "whole")
+        rest = held([P, 2, N // P, HALF], F32, "rest")
+        result = held([P, 2, N // P, HALF], F32, "result")
+        out_rows = out.rearrange("(i p) j -> p i j", p=P)
+
+        def finish(h, rows):
+            nc.vector.tensor_copy(whole[:, h, rows, :], angle[:, h, rows, :])
+            nc.vector.tensor_tensor(rest[:, h, rows, :], angle[:, h, rows, :], whole[:, h, rows, :], ALU.subtract)
+            nc.scalar.activation(result[:, h, rows, :], rest[:, h, rows, :], ACT.Sin, scale=2.0 * math.pi)
+            nc.sync.dma_start(out_rows[:, rows, h * HALF : (h + 1) * HALF], result[:, h, rows, :])
 
         for h in range(2):
             cols = slice(h * HALF, (h + 1) * HALF)
@@ -246,12 +272,8 @@ def tile_list_hologram_label_phase_kernel(
                     y, lhsT=w4_codes[:, 1, cols_of(i)].bitcast(FP8X4), lhsT_scale=w4_plane[4:, cols_of(i)],
                     rhs=z1[h][0][:].bitcast(FP8X4), rhs_scale=z1[h][1][:], start=False, stop=True,
                 )
-                whole = ring.tile([P, HALF], I32, name="whole")
-                nc.vector.tensor_scalar(whole[:], y, TURN, turns[:, i : i + 1], ALU.mult, ALU.add)
-                rest = ring.tile([P, HALF], F32, name="rest")
-                nc.vector.scalar_tensor_tensor(rest[:], y, TURN, whole[:], ALU.mult, ALU.subtract)
-                size = ring.tile([P, HALF], F32, name="size")
-                nc.scalar.activation(size[:], rest[:], ACT.Abs, bias=turns[:, i : i + 1])
-                result = ring.tile([P, HALF], F32, name="result")
-                nc.scalar.activation(result[:], size[:], ACT.Sin, bias=math.pi / 2, scale=-2.0 * math.pi)
-                nc.sync.dma_start(out[cols_of(i), cols], result[:])
+                nc.scalar.activation(angle[:, h, i, :], y, ACT.Identity, bias=turns[:, i : i + 1], scale=TURN)
+                if h == 1:
+                    finish(h, slice(i, i + 1))
+            if h == 0:
+                finish(h, slice(0, N // P))

@@ -68,17 +68,21 @@ def tile_list_hologram_label_phase_kernel(
             nc.sync.dma_start(raw[:], rows.rearrange("(p j) c -> p j c", j=PACK))
             return raw
 
-        def gather_bytes(window, lst, dtype, name):
-            picked = held([P, S], dtype, name)
+        def gather_bytes(window, lst, dtype, name, picked=None):
+            if picked is None:
+                picked = held([P, S], dtype, name)
             nc.vector.tensor_copy(picked[:], window[:].indirect(lst[:]))
             return picked
 
-        def quantise_weight(raw, name, grouped_tag, tag=None):
+        def cast_weight(copy, raw, name, grouped_tag):
             grouped = held([P, PASS * PACK], BF16, name + "_grouped", grouped_tag)
-            nc.scalar.copy(
+            copy(
                 grouped[:].rearrange("p (t m j) -> p m j t", t=PACK, j=PACK),
                 raw[:].rearrange("p j (m t) -> p m j t", t=PACK),
             )
+            return grouped
+
+        def quantise(grouped, name, tag=None):
             codes = held([P, PASS], U32, name + "_codes", tag)
             plane = held([P, PASS], U8, name + "_plane")
             nc.vector.quantize_mx(codes[:].bitcast(FP8X4), plane[:], grouped[:])
@@ -151,8 +155,11 @@ def tile_list_hologram_label_phase_kernel(
             w2_plane[:].rearrange("p (b t q) -> p b q t", b=2, t=PACK),
             w2_plane_raw[:].rearrange("p (b q t) -> p b q t", b=2, t=PACK),
         )
-        picked_plane3 = gather_bytes(plane3, list3, U8, "picked_plane3")
-        quant3 = [quantise_weight(raw3[b], f"w3_{b}", f"grouped{b}", tag) for b, tag in enumerate(("w2_plane_raw", "plane3"))]
+        grouped3 = [cast_weight(nc.vector.tensor_copy, raw3[0], "w3_0", "w2_plane_raw"),
+                    cast_weight(nc.scalar.copy, raw3[1], "w3_1", "grouped1")]
+        picked_plane3 = gather_bytes(plane3, list3, U8, "picked_plane3",
+                                     stage.tile([P, S], U8, name="picked_plane3", offset=0, align_bytes=64))
+        quant3 = [quantise(grouped3[0], "w3_0"), quantise(grouped3[1], "w3_1", "plane3")]
         picked3 = gather_bytes(words3, list3, U32, "picked3")
         picked_plane1 = gather_bytes(plane1, list1, U8, "picked_plane1")
         picked1 = [gather_bytes(words1[a], list1, U32, f"picked1_{a}") for a in range(2)]
@@ -168,7 +175,7 @@ def tile_list_hologram_label_phase_kernel(
             window = first_stage(
                 [(w2_codes[:, 2 * c0 : 2 * (c0 + P)].bitcast(FP4X4), w2_plane[:, c0 : c0 + P], picked2, picked_plane2)],
                 ACT.Copy, 0.0,
-                stage.tile([P, S], F32, name="first_window", offset=2 * 4 * S) if c0 == 0 else None,
+                stage.tile([P, S], F32, name="extra_window", offset=4 * S) if c0 == 7 * P else None,
             )
             nc.vector.tensor_copy(part_b[b][:, t, :], window[:].indirect(places2[:]))
 
@@ -188,7 +195,7 @@ def tile_list_hologram_label_phase_kernel(
                 part_d[b, t] = both[:, e, :]
                 nc.vector.tensor_tensor(part_d[b, t], windows_d[2 * pair + e][:].indirect(places3[:]), part_b[b][:, t, :], ALU.subtract)
             for a, b in (((0, 0), (1, 0)), ((0, 1),), ((1, 1),), ())[pair]:
-                quant1[a, b] = quantise_weight(raw1[a, b], f"w1_{a}{b}", f"grouped{2 * b + a}")
+                quant1[a, b] = quantise(cast_weight(nc.scalar.copy, raw1[a, b], f"w1_{a}{b}", f"grouped{2 * b + a}"), f"w1_{a}{b}")
 
         def a_window(b, t):
             return first_stage(
@@ -232,16 +239,13 @@ def tile_list_hologram_label_phase_kernel(
                     sums1[:, t, :], windows1[t][:].indirect(places1[:, h * HALF // 16 : (h + 1) * HALF // 16]),
                     part_d[1, t][:, cols], ALU.add,
                 )
-            if h == 0:
-                z = z_on_scalar(sums1, 1, HALF, "z1_0")
-            else:
-                z = held([P, HALF * PACK], BF16, f"z1_{h}")
-                nc.vector.tensor_tensor(
-                    z[:].rearrange("p (c i t) -> p c t i", i=4, t=PACK),
-                    sums1[:].rearrange("p t (c i) -> p c t i", i=4),
-                    gains[:, 1, :].unsqueeze(1).unsqueeze(3).to_broadcast([P, HALF // 4, PACK, 4]),
-                    ALU.mult,
-                )
+            z = held([P, HALF * PACK], BF16, f"z1_{h}")
+            nc.vector.tensor_tensor(
+                z[:].rearrange("p (c i t) -> p c t i", i=4, t=PACK),
+                sums1[:].rearrange("p t (c i) -> p c t i", i=4),
+                gains[:, 1, :].unsqueeze(1).unsqueeze(3).to_broadcast([P, HALF // 4, PACK, 4]),
+                ALU.mult,
+            )
             codes = held([P, HALF], U32, f"z1_codes_{h}")
             plane = held([P, HALF], U8, f"z1_plane_{h}")
             nc.vector.quantize_mx(codes[:].bitcast(FP8X4), plane[:], z[:])

@@ -82,6 +82,15 @@ def tile_list_hologram_label_phase_kernel(
             )
             return grouped
 
+        def cast_on_gpsimd(raw, name, grouped_tag):
+            grouped = held([P, PASS * PACK], BF16, name + "_grouped", grouped_tag)
+            nc.gpsimd.tensor_scalar(
+                grouped[:].rearrange("p (t m j) -> p m t j", t=PACK, j=PACK),
+                raw[:].rearrange("p j (m t) -> p m t j", t=PACK),
+                1.0, 0.0, ALU.mult, ALU.add,
+            )
+            return grouped
+
         def quantise(grouped, name, tag=None):
             codes = held([P, PASS], U32, name + "_codes", tag)
             plane = held([P, PASS], U8, name + "_plane")
@@ -113,26 +122,27 @@ def tile_list_hologram_label_phase_kernel(
         nc.scalar.activation(zero[:], zero_in[:], ACT.Silu)
 
         list2 = load_list(offs2, "list2")
-        w2_raw = held([P, 2 * H], U8, "w2_raw")
-        nc.sync.dma_start(w2_raw[:].bitcast(I32), w2_words[0].bitcast(I32))
         plane2 = held([P, T], U8, "plane2")
         for q in range(4):
             rows = tab2_scales[0, 4 * q : 4 * q + 4, :].bitcast(I32)
             nc.sync.dma_start(plane2[32 * q : 32 * q + 32, :].bitcast(I32), rows.unsqueeze(0).to_broadcast([8, 4, T // 4]))
         words2 = load_words(tab2_words, 0, "words2")
-        raw3 = [load_weight(w3, 0, 0, "raw3_0", 0)]
         load_plane(nc.sync, w2_plane_raw, w2_scales)
+        places2 = load_list(pos2, "places2")
+        w2_raw = held([P, 2 * H], U8, "w2_raw")
+        nc.sync.dma_start(w2_raw[:].bitcast(I32), w2_words[0].bitcast(I32))
+        raw3 = [load_weight(w3, 0, b, f"raw3_{b}", b) for b in range(2)]
         list3 = load_list(offs3, "list3")
-        raw3.append(load_weight(w3, 0, 1, "raw3_1", 1))
         load_plane(nc.sync, plane3, tab3_scales)
         words3 = load_words(tab3_words, 0, "words3")
-        places2 = load_list(pos2, "places2")
         list1 = load_list(offs, "list1")
         load_plane(nc.sync, plane1, tab_scales)
+        raw1 = {(a, 0): load_weight(w1, a, 0, f"raw1_{a}0", 2 + a) for a in range(2)}
         words1 = [load_words(tab_words, 0, "words1_0")]
         places3 = load_list(pos3, "places3")
+        for a in range(2):
+            raw1[a, 1] = load_weight(w1, a, 1, f"raw1_{a}1", 4 + a)
         words1.append(load_words(tab_words, 1, "words1_1"))
-        raw1 = {(a, b): load_weight(w1, a, b, f"raw1_{a}{b}", 2 + 2 * b + a) for b in range(2) for a in range(2)}
         places1 = load_list(pos1, "places1")
         gains = keep.tile([P, 2, PACK], F32, name="gains")
         nc.sync.dma_start(gains[:], gain.rearrange("(b p t) -> p b t", b=2, t=PACK))
@@ -143,13 +153,13 @@ def tile_list_hologram_label_phase_kernel(
         with nc.allow_non_contiguous_dma(reason="one phase a partition"):
             nc.sync.dma_start(phases[:], phase.rearrange("(i p) -> p i", p=P))
 
+        picked_plane2 = gather_bytes(plane2, list2, U8, "picked_plane2")
+        picked2 = gather_bytes(words2, list2, U32, "picked2")
         w2_codes = held([P, 2 * H], U8, "w2_codes")
         nc.vector.tensor_copy(
             w2_codes[:].bitcast(U16).rearrange("p (b t q) -> p b q t", b=2, t=PACK),
             w2_raw[:].bitcast(U16).rearrange("p (b q t) -> p b q t", b=2, t=PACK),
         )
-        picked_plane2 = gather_bytes(plane2, list2, U8, "picked_plane2")
-        picked2 = gather_bytes(words2, list2, U32, "picked2")
         w2_plane = held([P, H], U8, "w2_plane")
         nc.vector.tensor_copy(
             w2_plane[:].rearrange("p (b t q) -> p b q t", b=2, t=PACK),
@@ -157,45 +167,49 @@ def tile_list_hologram_label_phase_kernel(
         )
         grouped3 = [cast_weight(nc.vector.tensor_copy, raw3[0], "w3_0", "w2_plane_raw"),
                     cast_weight(nc.scalar.copy, raw3[1], "w3_1", "grouped1")]
-        picked_plane3 = gather_bytes(plane3, list3, U8, "picked_plane3",
-                                     stage.tile([P, S], U8, name="picked_plane3", offset=0, align_bytes=64))
-        quant3 = [quantise(grouped3[0], "w3_0"), quantise(grouped3[1], "w3_1", "plane3")]
-        picked3 = gather_bytes(words3, list3, U32, "picked3")
-        picked_plane1 = gather_bytes(plane1, list1, U8, "picked_plane1")
-        picked1 = [gather_bytes(words1[a], list1, U32, f"picked1_{a}") for a in range(2)]
+        quant3 = [quantise(grouped3[0], "w3_0")]
 
         slices = [(b, t) for b in range(2) for t in range(PACK)]
 
         def cols_of(t):
             return slice(t * P, (t + 1) * P)
 
-        part_b = [keep.tile([P, PACK, J], F32, name=f"part_b{b}", tag=tag, align_bytes=64) for b, tag in enumerate(("words3", "words1_0"))]
-        for b, t in slices:
+        def b_part(part, b, t):
             c0 = b * PASS + t * P
             window = first_stage(
                 [(w2_codes[:, 2 * c0 : 2 * (c0 + P)].bitcast(FP4X4), w2_plane[:, c0 : c0 + P], picked2, picked_plane2)],
                 ACT.Copy, 0.0,
-                stage.tile([P, S], F32, name="extra_window", offset=4 * S) if c0 == 7 * P else None,
+                stage.tile([P, S], F32, name=f"window_b{t}", offset=(t - 2) * 4 * S) if b == 0 and t >= 2 else None,
             )
-            nc.vector.tensor_copy(part_b[b][:, t, :], window[:].indirect(places2[:]))
+            nc.vector.tensor_copy(part[:, t, :], window[:].indirect(places2[:]))
 
-        windows_d = []
-        for b, t in slices:
-            codes, plane = quant3[b]
-            windows_d.append(first_stage(
-                [(codes[:, cols_of(t)].bitcast(FP8X4), plane[:, cols_of(t)], picked3, picked_plane3)],
-                ACT.Square, 0.0,
-            ))
-        quant1 = {}
+        part_b = [held([P, PACK, J], F32, "part_b0")]
+        for t in range(PACK):
+            b_part(part_b[0], 0, t)
+        picked_plane3 = gather_bytes(plane3, list3, U8, "picked_plane3",
+                                     stage.tile([P, S], U8, name="picked_plane3", offset=0, align_bytes=64))
+        picked3 = gather_bytes(words3, list3, U32, "picked3",
+                               stage.tile([P, S], U32, name="picked3", offset=4 * S, align_bytes=64))
+        quant3.append(quantise(grouped3[1], "w3_1", "plane3"))
+        picked_plane1 = gather_bytes(plane1, list1, U8, "picked_plane1", held([P, S], U8, "picked_plane1", "words3"))
+        quant1 = {(a, b): quantise(cast_on_gpsimd(raw1[a, b], f"w1_{a}{b}", f"grouped{2 * b + a}"), f"w1_{a}{b}")
+                  for b in range(2) for a in range(2)}
+        picked1 = [gather_bytes(words1[a], list1, U32, f"picked1_{a}") for a in range(2)]
+        part_b.append(held([P, PACK, J], F32, "part_b1", "words1_0"))
+        for t in range(PACK):
+            b_part(part_b[1], 1, t)
+
         part_d = {}
-        for pair, tag in enumerate(("words1_1", "grouped1", "grouped2", "grouped3")):
-            both = held([P, 2, J], F32, f"part_d{pair}", tag)
-            for e in range(2):
-                b, t = slices[2 * pair + e]
-                part_d[b, t] = both[:, e, :]
-                nc.vector.tensor_tensor(part_d[b, t], windows_d[2 * pair + e][:].indirect(places3[:]), part_b[b][:, t, :], ALU.subtract)
-            for a, b in (((0, 0), (1, 0)), ((0, 1),), ((1, 1),), ())[pair]:
-                quant1[a, b] = quantise(cast_weight(nc.scalar.copy, raw1[a, b], f"w1_{a}{b}", f"grouped{2 * b + a}"), f"w1_{a}{b}")
+        for b, tag in enumerate(("words1_1", "words2")):
+            four = held([P, PACK, J], F32, f"part_d{b}", tag)
+            codes, plane = quant3[b]
+            for t in range(PACK):
+                window = first_stage(
+                    [(codes[:, cols_of(t)].bitcast(FP8X4), plane[:, cols_of(t)], picked3, picked_plane3)],
+                    ACT.Square, 0.0,
+                )
+                part_d[b, t] = four[:, t, :]
+                nc.vector.tensor_tensor(part_d[b, t], window[:].indirect(places3[:]), part_b[b][:, t, :], ALU.subtract)
 
         def a_window(b, t):
             return first_stage(
@@ -239,19 +253,22 @@ def tile_list_hologram_label_phase_kernel(
                     sums1[:, t, :], windows1[t][:].indirect(places1[:, h * HALF // 16 : (h + 1) * HALF // 16]),
                     part_d[1, t][:, cols], ALU.add,
                 )
-            z = held([P, HALF * PACK], BF16, f"z1_{h}")
-            nc.vector.tensor_tensor(
-                z[:].rearrange("p (c i t) -> p c t i", i=4, t=PACK),
-                sums1[:].rearrange("p t (c i) -> p c t i", i=4),
-                gains[:, 1, :].unsqueeze(1).unsqueeze(3).to_broadcast([P, HALF // 4, PACK, 4]),
-                ALU.mult,
-            )
+            if h == 0:
+                z = z_on_scalar(sums1, 1, HALF, "z1_0")
+            else:
+                z = held([P, HALF * PACK], BF16, f"z1_{h}")
+                nc.vector.tensor_tensor(
+                    z[:].rearrange("p (c i t) -> p c t i", i=4, t=PACK),
+                    sums1[:].rearrange("p t (c i) -> p c t i", i=4),
+                    gains[:, 1, :].unsqueeze(1).unsqueeze(3).to_broadcast([P, HALF // 4, PACK, 4]),
+                    ALU.mult,
+                )
             codes = held([P, HALF], U32, f"z1_codes_{h}")
             plane = held([P, HALF], U8, f"z1_plane_{h}")
             nc.vector.quantize_mx(codes[:].bitcast(FP8X4), plane[:], z[:])
             z1.append((codes, plane))
 
-        angle = held([P, 2, N // P, HALF], F32, "angle", "words2")
+        angle = held([P, 2, N // P, HALF], F32, "angle", "words1_0")
         whole = held([P, 2, N // P, HALF], I32, "whole")
         rest = held([P, 2, N // P, HALF], F32, "rest")
         result = held([P, 2, N // P, HALF], F32, "result")

import math
from contextlib import ExitStack

import concourse.mybir as mybir

K, K2, K3, T, S, H, N, J = 1024, 512, 512, 2048, 1024, 1024, 384, 512
FLOPS = 2 * (K + K2 + K3) * H * S + 2 * H * N * J

F32 = mybir.dt.float32
BF16 = mybir.dt.bfloat16
I32 = mybir.dt.int32
U32 = mybir.dt.uint32
U16 = mybir.dt.uint16
U8 = mybir.dt.uint8
FP8X4 = mybir.dt.float8_e4m3fn_x4
FP4X4 = mybir.dt.float4_e2m1fn_x4
ACT = mybir.ActivationFunctionType
ALU = mybir.AluOpType

P = 128
PACK = 4
PASS = P * PACK
BANK = 512
HALF = J // 2
TURN = 1.0 / (2.0 * math.pi)
QUARTER = 0.25


def tile_list_hologram_label_phase_kernel(
    tc, tab_words, tab_scales, tab2_words, tab2_scales, tab3_words, tab3_scales,
    offs, offs2, offs3, pos1, pos2, pos3, w1, w2_words, w2_scales, w3, gain,
    w4_words, w4_scales, phase, out,
):
    nc = tc.nc
    with ExitStack() as ctx:
        keep = ctx.enter_context(tc.tile_pool(name="keep", bufs=1))
        ring = ctx.enter_context(tc.tile_pool(name="ring", bufs=3))
        stage = ctx.enter_context(tc.tile_pool(name="stage", bufs=1))
        psum = ctx.enter_context(tc.psum_pool(name="psum", bufs=8))

        def held(shape, dtype, name, tag=None):
            return keep.tile(shape, dtype, name=name, tag=tag or name, align_bytes=64)

        def load_list(dram, name):
            lst = keep.tile(list(dram.shape), U16, name=name)
            nc.sync.dma_start(lst[:], dram)
            return lst

        def zeroed_plane(engine, width, name):
            plane = held([P, width], U8, name)
            engine.memset(plane[:].bitcast(I32), 0)
            return plane

        def load_plane(queue, plane, scales):
            passes = scales.shape[0]
            for q in range(4):
                rows = scales[:, 4 * q : 4 * q + 4, :] if passes > 1 else scales[0, 4 * q : 4 * q + 4, :]
                queue.dma_start(plane[32 * q : 32 * q + 4 * passes, :].bitcast(I32), rows.bitcast(I32))

        def load_words(words, a, name):
            tile = keep.tile([P, T], U32, name=name, tag=name, align_bytes=64)
            nc.sync.dma_start(tile[:].bitcast(I32), words[a].rearrange("p t i -> p (t i)").bitcast(I32))
            return tile

        def load_weight(w, a, b, name, place):
            raw = stage.tile([P, PACK, PASS], F32, name=name, offset=place * 2 * 4 * S)
            rows = w[a * PASS : (a + 1) * PASS, b * PASS : (b + 1) * PASS]
            nc.sync.dma_start(raw[:], rows.rearrange("(p j) c -> p j c", j=PACK))
            return raw

        def gather_bytes(window, lst, dtype, name, picked=None):
            if picked is None:
                picked = held([P, S], dtype, name)
            nc.vector.tensor_copy(picked[:], window[:].indirect(lst[:]))
            return picked

        def cast_weight(copy, raw, name, grouped_tag):
            grouped = held([P, PASS * PACK], BF16, name + "_grouped", grouped_tag)
            copy(
                grouped[:].rearrange("p (t m j) -> p m j t", t=PACK, j=PACK),
                raw[:].rearrange("p j (m t) -> p m j t", t=PACK),
            )
            return grouped

        def cast_on_gpsimd(raw, name, grouped_tag):
            grouped = held([P, PASS * PACK], BF16, name + "_grouped", grouped_tag)
            nc.gpsimd.tensor_scalar(
                grouped[:].rearrange("p (t m j) -> p m t j", t=PACK, j=PACK),
                raw[:].rearrange("p j (m t) -> p m t j", t=PACK),
                1.0, 0.0, ALU.mult, ALU.add,
            )
            return grouped

        def quantise(grouped, name, tag=None):
            codes = held([P, PASS], U32, name + "_codes", tag)
            plane = held([P, PASS], U8, name + "_plane")
            nc.vector.quantize_mx(codes[:].bitcast(FP8X4), plane[:], grouped[:])
            return codes, plane

        def first_stage(passes, func, bias, window=None):
            if window is None:
                window = ring.tile([P, S], F32, name="window", bufs=8)
            for h in range(S // BANK):
                cols = slice(h * BANK, (h + 1) * BANK)
                acc = psum.tile([P, BANK], F32, name="acc")
                for a, (lhs, lhs_plane, words, plane) in enumerate(passes):
                    nc.tensor.matmul_mx(
                        acc[:], lhsT=lhs, lhsT_scale=lhs_plane,
                        rhs=words[:, cols].bitcast(FP8X4), rhs_scale=plane[4 * a :, cols],
                        start=(a == 0), stop=(a == len(passes) - 1),
                    )
                nc.scalar.activation(window[:, cols], acc[:], func, bias=bias)
            return window

        w2_plane_raw = zeroed_plane(nc.vector, H, "w2_plane_raw")
        plane3 = zeroed_plane(nc.vector, T, "plane3")
        plane1 = zeroed_plane(nc.vector, T, "plane1")
        w4_plane = zeroed_plane(nc.vector, N, "w4_plane")
        zero_in = keep.tile([P, 1], F32, name="zero_in")
        nc.vector.memset(zero_in[:], 0.0)
        zero = keep.tile([P, 1], F32, name="zero")
        nc.scalar.activation(zero[:], zero_in[:], ACT.Silu)

        list2 = load_list(offs2, "list2")
        plane2 = held([P, T], U8, "plane2")
        for q in range(4):
            rows = tab2_scales[0, 4 * q : 4 * q + 4, :].bitcast(I32)
            nc.sync.dma_start(plane2[32 * q : 32 * q + 32, :].bitcast(I32), rows.unsqueeze(0).to_broadcast([8, 4, T // 4]))
        words2 = load_words(tab2_words, 0, "words2")
        load_plane(nc.sync, w2_plane_raw, w2_scales)
        places2 = load_list(pos2, "places2")
        w2_raw = held([P, 2 * H], U8, "w2_raw")
        nc.sync.dma_start(w2_raw[:].bitcast(I32), w2_words[0].bitcast(I32))
        raw3 = [load_weight(w3, 0, b, f"raw3_{b}", b) for b in range(2)]
        list3 = load_list(offs3, "list3")
        load_plane(nc.sync, plane3, tab3_scales)
        words3 = load_words(tab3_words, 0, "words3")
        list1 = load_list(offs, "list1")
        load_plane(nc.sync, plane1, tab_scales)
        raw1 = {(a, 0): load_weight(w1, a, 0, f"raw1_{a}0", 2 + a) for a in range(2)}
        words1 = [load_words(tab_words, 0, "words1_0")]
        places3 = load_list(pos3, "places3")
        for a in range(2):
            raw1[a, 1] = load_weight(w1, a, 1, f"raw1_{a}1", 4 + a)
        words1.append(load_words(tab_words, 1, "words1_1"))
        places1 = load_list(pos1, "places1")
        gains = keep.tile([P, 2, PACK], F32, name="gains")
        nc.sync.dma_start(gains[:], gain.rearrange("(b p t) -> p b t", b=2, t=PACK))
        w4_codes = held([P, 2, N], U32, "w4_codes")
        nc.sync.dma_start(w4_codes[:].bitcast(I32), w4_words.rearrange("a p n i -> p a (n i)").bitcast(I32))
        load_plane(nc.sync, w4_plane, w4_scales)
        phases = keep.tile([P, N // P], F32, name="phases")
        with nc.allow_non_contiguous_dma(reason="one phase a partition"):
            nc.sync.dma_start(phases[:], phase.rearrange("(i p) -> p i", p=P))

        picked_plane2 = gather_bytes(plane2, list2, U8, "picked_plane2")
        picked2 = gather_bytes(words2, list2, U32, "picked2")
        w2_codes = held([P, 2 * H], U8, "w2_codes")
        nc.vector.tensor_copy(
            w2_codes[:].bitcast(U16).rearrange("p (b t q) -> p b q t", b=2, t=PACK),
            w2_raw[:].bitcast(U16).rearrange("p (b q t) -> p b q t", b=2, t=PACK),
        )
        w2_plane = held([P, H], U8, "w2_plane")
        nc.vector.tensor_copy(
            w2_plane[:].rearrange("p (b t q) -> p b q t", b=2, t=PACK),
            w2_plane_raw[:].rearrange("p (b q t) -> p b q t", b=2, t=PACK),
        )
        grouped3 = [cast_weight(nc.vector.tensor_copy, raw3[0], "w3_0", "w2_plane_raw"),
                    cast_weight(nc.scalar.copy, raw3[1], "w3_1", "grouped1")]
        quant3 = [quantise(grouped3[0], "w3_0")]

        slices = [(b, t) for b in range(2) for t in range(PACK)]

        def cols_of(t):
            return slice(t * P, (t + 1) * P)

        def b_part(part, b, t):
            c0 = b * PASS + t * P
            window = first_stage(
                [(w2_codes[:, 2 * c0 : 2 * (c0 + P)].bitcast(FP4X4), w2_plane[:, c0 : c0 + P], picked2, picked_plane2)],
                ACT.Copy, 0.0,
                stage.tile([P, S], F32, name=f"window_b{t}", offset=(t - 2) * 4 * S) if b == 0 and t >= 2 else None,
            )
            nc.vector.tensor_copy(part[:, t, :], window[:].indirect(places2[:]))

        part_b = [held([P, PACK, J], F32, "part_b0")]
        for t in range(PACK):
            b_part(part_b[0], 0, t)
        picked_plane3 = gather_bytes(plane3, list3, U8, "picked_plane3",
                                     stage.tile([P, S], U8, name="picked_plane3", offset=0, align_bytes=64))
        picked3 = gather_bytes(words3, list3, U32, "picked3",
                               stage.tile([P, S], U32, name="picked3", offset=4 * S, align_bytes=64))
        quant3.append(quantise(grouped3[1], "w3_1", "plane3"))
        picked_plane1 = gather_bytes(plane1, list1, U8, "picked_plane1", held([P, S], U8, "picked_plane1", "words3"))
        quant1 = {(a, b): quantise(cast_on_gpsimd(raw1[a, b], f"w1_{a}{b}", f"grouped{2 * b + a}"), f"w1_{a}{b}")
                  for b in range(2) for a in range(2)}
        picked1 = [gather_bytes(words1[a], list1, U32, f"picked1_{a}") for a in range(2)]
        part_b.append(held([P, PACK, J], F32, "part_b1", "words1_0"))
        for t in range(PACK):
            b_part(part_b[1], 1, t)

        part_d = {}
        for b, tag in enumerate(("words1_1", "words2")):
            four = held([P, PACK, J], F32, f"part_d{b}", tag)
            codes, plane = quant3[b]
            for t in range(PACK):
                window = first_stage(
                    [(codes[:, cols_of(t)].bitcast(FP8X4), plane[:, cols_of(t)], picked3, picked_plane3)],
                    ACT.Square, 0.0,
                )
                part_d[b, t] = four[:, t, :]
                nc.vector.tensor_tensor(part_d[b, t], window[:].indirect(places3[:]), part_b[b][:, t, :], ALU.subtract)

        def a_window(b, t):
            return first_stage(
                [(quant1[a, b][0][:, cols_of(t)].bitcast(FP8X4), quant1[a, b][1][:, cols_of(t)], picked1[a], picked_plane1)
                 for a in range(2)],
                ACT.Tanh, zero[:],
                stage.tile([P, S], F32, name=f"window_a{b}{t}", offset=(10 - 4 * b - 2 * (t // 2) + t % 2) * 4 * S),
            )

        sums0 = keep.tile([P, PACK, J], F32, name="sums0")
        for t in range(PACK):
            window = a_window(0, t)
            nc.vector.tensor_tensor(sums0[:, t, :], window[:].indirect(places1[:]), part_d[0, t], ALU.add)
        windows1 = [a_window(1, t) for t in range(PACK)]

        def z_on_scalar(sums, b, width, name):
            scaled = held([P, PACK, width], BF16, name + "_scaled")
            for t in range(PACK):
                nc.scalar.activation(scaled[:, t, :], sums[:, t, :], ACT.Copy, scale=gains[:, b, t : t + 1])
            z = held([P, width * PACK], BF16, name)
            nc.scalar.copy(
                z[:].rearrange("p (c i t) -> p c t i", i=4, t=PACK),
                scaled[:].rearrange("p t (c i) -> p c t i", i=4),
            )
            return z

        z0 = z_on_scalar(sums0, 0, J, "z0")
        z0_codes = held([P, J], U32, "z0_codes")
        z0_plane = held([P, J], U8, "z0_plane")
        nc.vector.quantize_mx(z0_codes[:].bitcast(FP8X4), z0_plane[:], z0[:])

        turns = keep.tile([P, N // P], F32, name="turns")
        nc.vector.tensor_scalar(turns[:], phases[:], TURN, QUARTER, ALU.mult, ALU.add)

        z1 = []
        for h in range(2):
            cols = slice(h * HALF, (h + 1) * HALF)
            sums1 = keep.tile([P, PACK, HALF], F32, name=f"sums1_{h}")
            for t in range(PACK):
                nc.vector.tensor_tensor(
                    sums1[:, t, :], windows1[t][:].indirect(places1[:, h * HALF // 16 : (h + 1) * HALF // 16]),
                    part_d[1, t][:, cols], ALU.add,
                )
            if h == 0:
                z = z_on_scalar(sums1, 1, HALF, "z1_0")
            else:
                z = held([P, HALF * PACK], BF16, f"z1_{h}")
                nc.vector.tensor_tensor(
                    z[:].rearrange("p (c i t) -> p c t i", i=4, t=PACK),
                    sums1[:].rearrange("p t (c i) -> p c t i", i=4),
                    gains[:, 1, :].unsqueeze(1).unsqueeze(3).to_broadcast([P, HALF // 4, PACK, 4]),
                    ALU.mult,
                )
            codes = held([P, HALF], U32, f"z1_codes_{h}")
            plane = held([P, HALF], U8, f"z1_plane_{h}")
            nc.vector.quantize_mx(codes[:].bitcast(FP8X4), plane[:], z[:])
            z1.append((codes, plane))

        angle = held([P, 2, N // P, HALF], F32, "angle", "words1_0")
        whole = held([P, 2, N // P, HALF], I32, "whole")
        rest = held([P, 2, N // P, HALF], F32, "rest")
        result = held([P, 2, N // P, HALF], F32, "result")
        out_rows = out.rearrange("(i p) j -> p i j", p=P)

        def finish(h, rows):
            nc.vector.tensor_copy(whole[:, h, rows, :], angle[:, h, rows, :])
            nc.vector.tensor_tensor(rest[:, h, rows, :], angle[:, h, rows, :], whole[:, h, rows, :], ALU.subtract)
            nc.scalar.activation(result[:, h, rows, :], rest[:, h, rows, :], ACT.Sin, scale=2.0 * math.pi)
            nc.sync.dma_start(out_rows[:, rows, h * HALF : (h + 1) * HALF], result[:, h, rows, :])

        for h in range(2):
            cols = slice(h * HALF, (h + 1) * HALF)
            for i in range(N // P):
                acc = psum.tile([P, BANK], F32, name="acc")
                y = acc[:, :HALF]
                nc.tensor.matmul_mx(
                    y, lhsT=w4_codes[:, 0, cols_of(i)].bitcast(FP8X4), lhsT_scale=w4_plane[:, cols_of(i)],
                    rhs=z0_codes[:, cols].bitcast(FP8X4), rhs_scale=z0_plane[:, cols], start=True, stop=False,
                )
                nc.tensor.matmul_mx(
                    y, lhsT=w4_codes[:, 1, cols_of(i)].bitcast(FP8X4), lhsT_scale=w4_plane[4:, cols_of(i)],
                    rhs=z1[h][0][:].bitcast(FP8X4), rhs_scale=z1[h][1][:], start=False, stop=True,
                )
                nc.scalar.activation(angle[:, h, i, :], y, ACT.Identity, bias=turns[:, i : i + 1], scale=TURN)
                if h == 1:
                    finish(h, slice(i, i + 1))
            if h == 0:
                finish(h, slice(0, N // P))
